import numpy as np
import ml_dtypes


def mxq(x, axis, fmt="e4m3"):
    dtype, down = {"e4m3": (ml_dtypes.float8_e4m3fn, 7), "e5m2": (ml_dtypes.float8_e5m2, 14)}[fmt]
    v = np.moveaxis(np.asarray(x, np.float32).astype(ml_dtypes.bfloat16).astype(np.float64), axis, -1)
    blocks = v.reshape(v.shape[:-1] + (-1, 32))
    amax = np.abs(blocks).max(-1, keepdims=True)
    byte = np.maximum(np.where(amax > 0, np.frexp(amax)[1] - 1 + 127, 0) - down, 1)
    scale = np.exp2(byte - 127.0)
    codes = (blocks / scale).astype(np.float32).astype(dtype).astype(np.float64)
    return np.moveaxis((codes * scale).reshape(v.shape), -1, axis)


WIDE = False


def mx_kscale(k):
    if not WIDE:
        return np.ones(k)
    levels = np.array([10, -10, 5, -5, 0])
    if k % 512:
        return np.exp2(np.random.permutation(np.resize(levels, k // 32))).repeat(32)
    a = np.empty((k // 512, 16))
    for p in range(k // 512):
        a[p, :8] = np.random.permutation(np.resize(levels, 8))
        for g in range(8):
            far = levels[np.abs(levels - a[p, g]) >= 10]
            a[p, g + 8] = far[np.random.randint(len(far))]
    return np.exp2(a.ravel()).repeat(32)


BF16 = ml_dtypes.bfloat16


def bf(x):
    return np.asarray(x, np.float32).astype(BF16)


def f64(x):
    return np.asarray(x).astype(np.float64)


E2M1 = np.array([0.0, 0.5, 1.0, 1.5, 2.0, 3.0, 4.0, 6.0, -0.0, -0.5, -1.0, -1.5, -2.0, -3.0, -4.0, -6.0])


def pack_weight(w, fmt):
    k, n = w.shape
    w = f64(bf(w)).reshape(k // 32, 32, n)
    amax = np.abs(w).max(1)
    if fmt == "e4m3":
        byte = np.frexp(amax)[1] - 1 + 127 - 7
    else:
        mant, ex = np.frexp(amax / 6.0)
        byte = np.where(mant > 0.5, ex, ex - 1) + 127
    byte = np.clip(np.where(amax > 0, byte, 1), 1, 254)
    scaled = (w * np.exp2(127.0 - byte)[:, None, :]).reshape(k, n).astype(np.float32)
    by_word = np.ascontiguousarray(scaled.reshape(k // 512, 128, 4, n).transpose(0, 1, 3, 2))
    if fmt == "e4m3":
        words = by_word.astype(ml_dtypes.float8_e4m3fn).view(np.uint8)
    else:
        c = by_word.astype(ml_dtypes.float4_e2m1fn).view(np.uint8) & 0xF
        words = c[..., 0::2] | (c[..., 1::2] << 4)
    return np.ascontiguousarray(words), np.ascontiguousarray(byte.astype(np.uint8).reshape(k // 512, 16, n))


def unpack_weight(words, scales, fmt):
    g, p, n, _ = words.shape
    if fmt == "e4m3":
        vals = np.ascontiguousarray(words).view(ml_dtypes.float8_e4m3fn).astype(np.float64)
    else:
        nib = np.empty((g, p, n, 4), np.uint8)
        nib[..., 0::2] = words & 0xF
        nib[..., 1::2] = words >> 4
        vals = E2M1[nib]
    vals = vals * np.repeat(np.exp2(scales.astype(np.float64) - 127.0), 8, axis=1)[..., None]
    return vals.transpose(0, 1, 3, 2).reshape(g * 512, n)
def pack4(w):
    words, scales = pack_weight(w, "e2m1")
    return words.reshape(words.shape[0], 128, -1), scales


def unpack4(words, scales):
    return unpack_weight(words.reshape(words.shape[0], 128, -1, 2), scales, "e2m1")


def planes(Y):
    n, m = Y.shape
    b = f64(bf(Y)).reshape(n // 32, 32, m)
    amax = np.abs(b).max(1)
    byte = np.clip(np.where(amax > 0, np.frexp(amax)[1] - 1 + 127 - 7, 1), 1, 254)
    codes = (b * np.exp2(127.0 - byte)[:, None, :]).reshape(n, m).astype(np.float32).astype(ml_dtypes.float8_e4m3fn).view(np.uint8)
    words = codes.reshape(n // 512, 128, 4, m).transpose(0, 1, 3, 2)
    return np.ascontiguousarray(words), np.ascontiguousarray(byte.astype(np.uint8).reshape(n // 512, 16, m))


T, J, P, R, Q = 256, 4, 512, 512, 1024


def setup_inputs():
    g, u = mx_kscale(P), mx_kscale(R)
    x = bf(np.random.standard_normal((T, J, P)) * g)
    a = bf(np.random.standard_normal((J, J)) / np.sqrt(J))
    b = bf(np.random.standard_normal((P, R)) / np.sqrt(P) / g[:, None] * u[None, :])
    e = bf(1.0 + 0.1 * np.random.standard_normal(R))
    c_words, c_scales = pack4(np.random.standard_normal((R, Q)) / np.sqrt(R) / u[:, None])
    s = bf(1.0 + 0.1 * np.random.standard_normal(Q))
    return {"x": x,
            "a": a,
            "b": b,
            "e": e,
            "c_words": c_words,
            "c_scales": c_scales,
            "s": s}


def mix_blocks(a, z):
    m = a[:, 0][None, :, None] * z[:, 0, :][:, None, :]
    for j in range(1, a.shape[1]):
        m = m + a[:, j][None, :, None] * z[:, j, :][:, None, :]
    return m


def core(x, a, b, e, c_words, c_scales, s):
    x, a, b, e, s = f64(x), f64(a), f64(b), f64(e), f64(s)
    c = unpack4(c_words, c_scales)
    t, j, p = x.shape
    q = c.shape[1]
    be = b * e[None, :]
    w2 = mxq(be, 1, "e4m3") @ c
    z = (mxq(x.reshape(t * j, p), 1, "e4m3") @ mxq(w2, 0, "e4m3")).reshape(t, j, q)
    m = mix_blocks(a, z)
    return m * s[None, None, :]


def reference(x, a, b, e, c_words, c_scales, s):
    R_out = core(x, a, b, e, c_words, c_scales, s)
    words, scales = planes(np.moveaxis(R_out, 2, 0).reshape(1024, -1))
    return R_out, words, scales

@@ -1,0 +1,346 @@
+from contextlib import ExitStack
+
+import concourse.mybir as mybir
+from concourse.masks import make_identity
+
+F32 = mybir.dt.float32
+BF16 = mybir.dt.bfloat16
+I32 = mybir.dt.int32
+U32 = mybir.dt.uint32
+U8 = mybir.dt.uint8
+E4M3 = mybir.dt.float8_e4m3fn_x4
+E2M1 = mybir.dt.float4_e2m1fn_x4
+ALU = mybir.AluOpType
+COPY = mybir.ActivationFunctionType.Copy
+
+T, J, P, R, Q = 256, 4, 512, 512, 1024
+FLOPS = 2 * P * R * Q + 2 * T * J * P * Q + 2 * T * J * J * Q
+
+UNITS = [(0, 0, 256), (1, 0, 128), (1, 128, 128)]
+DISP = [0, 4, 4, 4, 2, 2, 2, 2, 0, 0, 0, 0]
+
+
+def tile_lokrrankgatedkroneckerdelta_x2_kernel(tc, x, a, b, e, c_words, c_scales, s, out_0, out_1, out_2):
+    nc = tc.nc
+    with ExitStack() as ctx:
+        keep = ctx.enter_context(tc.tile_pool(name="keep", bufs=1))
+        opool = ctx.enter_context(tc.tile_pool(name="opool", bufs=8))
+        bpool = ctx.enter_context(tc.tile_pool(name="bpool", bufs=4))
+        psz = ctx.enter_context(tc.psum_pool(name="psz", bufs=6))
+        pst = ctx.enter_context(tc.psum_pool(name="pst", bufs=2))
+        ctx.enter_context(tc.manual_schedule())
+
+        b_in = keep.tile([128, 4, 512], BF16, name="b_in")
+        b_src = b.rearrange("(m t) r -> m t r", t=4)
+        e_col = keep.tile([128, 4], BF16, name="e_col")
+        s_col = keep.tile([128, 2, 4], BF16, name="s_col")
+        a_row = keep.tile([128, 16], BF16, name="a_row")
+        c_codes = keep.tile([128, 2 * Q], U8, name="c_codes", align_bytes=64)
+        c_plane = keep.tile([128, Q], U8, name="c_plane", align_bytes=64)
+        x_in = [keep.tile([128, 4, 512], BF16, name="x_in%d" % h) for h in range(2)]
+
+        nc.vector.memset(c_plane[:].bitcast(I32), 0)
+        nc.sync.dma_start(out=b_in[:, 0:2, :], in_=b_src[:, 0:2, :])
+        nc.sync.dma_start(out=b_in[:, 2:4, :], in_=b_src[:, 2:4, :])
+        nc.scalar.dma_start(out=e_col[:], in_=e.rearrange("(p k) -> p k", k=4))
+        nc.sync.dma_start(out=c_codes[:].bitcast(I32), in_=c_words[0].bitcast(I32))
+        for qd in range(4):
+            nc.scalar.dma_start(
+                out=c_plane[32 * qd : 32 * qd + 4, :].bitcast(I32),
+                in_=c_scales[0, 4 * qd : 4 * qd + 4, :].bitcast(I32),
+            )
+        nc.scalar.dma_start(out=s_col[:], in_=s.rearrange("(g p k) -> p g k", g=2, k=4))
+        nc.scalar.dma_start(out=a_row[:], in_=a.rearrange("i j -> (i j)").partition_broadcast(128))
+        for h in range(2):
+            for jp in range(2):
+                two = slice(2 * jp, 2 * jp + 2)
+                nc.sync.dma_start(out=x_in[h][:, two, :], in_=x[128 * h : 128 * h + 128, two, :])
+
+        ident = keep.tile([128, 128], F32, name="ident")
+        make_identity(nc, ident[:])
+
+        e_rep = keep.tile([128, 128, 4], BF16, name="e_rep")
+        nc.vector.tensor_copy(out=e_rep[:], in_=e_col[:].unsqueeze(1).to_broadcast([128, 128, 4]))
+        coef = keep.tile([128, 8, 16], F32, name="coef")
+        nc.vector.tensor_tensor(
+            out=coef[:],
+            in0=s_col[:].rearrange("p g k -> p (g k)").unsqueeze(2).to_broadcast([128, 8, 16]),
+            in1=a_row[:].unsqueeze(1).to_broadcast([128, 8, 16]),
+            op=ALU.mult,
+        )
+
+        be_words = keep.tile([128, 4, 128, 2], F32, name="be_words")
+        be_bf = keep.tile([128, 4, 512], BF16, name="be_bf", align_bytes=64)
+        be_codes = keep.tile([128, 512], U32, name="be_codes", align_bytes=64)
+        be_plane = keep.tile([128, 512], U8, name="be_plane", align_bytes=64)
+        for tp in range(2):
+            bank = psz.tile([128, 2, 2, 128], F32, name="z")
+            for t in range(2):
+                words = b_in[:, 2 * tp + t, :].bitcast(F32)
+                for u in range(2):
+                    nc.tensor.transpose(bank[:, t, u, :], words[:, u::2], ident[:])
+            nc.scalar.copy(out=be_words[:, 2 * tp : 2 * tp + 2, :, :], in_=bank[:].rearrange("p t u m -> p t m u"))
+            two = slice(2 * tp, 2 * tp + 2)
+            nc.vector.tensor_tensor(
+                out=be_bf[:, two, :],
+                in0=be_words[:, two, :, :].rearrange("p t m u -> p (t m u)").bitcast(BF16).rearrange("p (t c) -> p t c", t=2),
+                in1=e_rep[:].rearrange("p m k -> p (m k)").unsqueeze(1).to_broadcast([128, 2, 512]),
+                op=ALU.mult,
+            )
+        for tp in range(2):
+            two = slice(2 * tp, 2 * tp + 2)
+            cols = slice(256 * tp, 256 * tp + 256)
+            nc.vector.quantize_mx(
+                out=be_codes[:, cols].bitcast(E4M3),
+                scales=be_plane[:, cols],
+                in_=be_bf[:, two, :].rearrange("p t c -> p (t c)"),
+            )
+
+        x_words = keep.tile([128, 4, 256, 2], F32, name="x_words", align_bytes=64)
+        x_codes = keep.tile([128, 1024], U32, name="x_codes", align_bytes=64)
+        x_plane = keep.tile([128, 1024], U8, name="x_plane", align_bytes=64)
+
+        def x_turn(h, jps, pool, name):
+            for jp in jps:
+                bank = pool.tile([128, 2, 2, 128], F32, name=name)
+                for jj in range(2):
+                    words = x_in[h][:, 2 * jp + jj, :].bitcast(F32)
+                    for u in range(2):
+                        nc.tensor.transpose(bank[:, jj, u, :], words[:, u::2], ident[:])
+                nc.scalar.copy(
+                    out=x_words[:, 2 * jp : 2 * jp + 2, 128 * h : 128 * h + 128, :],
+                    in_=bank[:].rearrange("p j u t -> p j t u"),
+                )
+
+        def x_quant(h, js):
+            for j in js:
+                c0 = 256 * j + 128 * h
+                nc.vector.quantize_mx(
+                    out=x_codes[:, c0 : c0 + 128].bitcast(E4M3),
+                    scales=x_plane[:, c0 : c0 + 128],
+                    in_=x_words[:, j, 128 * h : 128 * h + 128, :].rearrange("p t u -> p (t u)").bitcast(BF16),
+                )
+
+        w_bf = [keep.tile([128, 4, 128, 4], BF16, name="w_bf%d" % g, align_bytes=64) for g in range(2)]
+        w_codes = [keep.tile([128, 512], U32, name="w_codes%d" % g, align_bytes=64) for g in range(2)]
+        w_plane = [keep.tile([128, 512], U8, name="w_plane%d" % g, align_bytes=64) for g in range(2)]
+
+        def w_block(g, blk, pool, name, on_vector):
+            bank = pool.tile([128, 4, 128], F32, name=name)
+            q0 = 512 * g + 128 * blk
+            for t in range(4):
+                nc.tensor.matmul_mx(
+                    out=bank[:, t, :],
+                    lhsT=be_codes[:, 128 * t : 128 * t + 128].bitcast(E4M3),
+                    lhsT_scale=be_plane[:, 128 * t : 128 * t + 128],
+                    rhs=c_codes[:, 2 * q0 : 2 * q0 + 256].bitcast(E2M1),
+                    rhs_scale=c_plane[:, q0 : q0 + 128],
+                    start=True,
+                    stop=True,
+                )
+            src = bank[:].rearrange("p t (x k) -> p k x t", k=4)
+            dst = w_bf[g][:, :, 32 * blk : 32 * blk + 32, :]
+            if on_vector:
+                nc.vector.tensor_copy(out=dst, in_=src)
+            else:
+                nc.scalar.copy(out=dst, in_=src)
+
+        def w_quant(g, k0, n):
+            cols = slice(128 * k0, 128 * (k0 + n))
+            nc.vector.quantize_mx(
+                out=w_codes[g][:, cols].bitcast(E4M3),
+                scales=w_plane[g][:, cols],
+                in_=w_bf[g][:, k0 : k0 + n, :, :].rearrange("p k x t -> p (k x t)"),
+            )
+
+        slots = [(u, k) for u in range(3) for k in range(4)]
+        m_tiles = [keep.tile([128, 4, 4, UNITS[u][2]], F32, name="m%d" % u) for u in range(3)]
+        zs = {}
+
+        def z_make(n):
+            u, k = slots[n]
+            g, t0, tn = UNITS[u]
+            per = 512 // tn
+            banks = []
+            for bk in range(4 // per):
+                bank = psz.tile([128, per, tn], F32, name="z")
+                if tn == 256:
+                    c0 = 512 * bk
+                    pieces = [(bank[:].rearrange("p j t -> p (j t)"), c0, 512)]
+                else:
+                    pieces = [(bank[:, j, :], 256 * j + t0, 128) for j in range(4)]
+                for dst, c0, w in pieces:
+                    nc.tensor.matmul_mx(
+                        out=dst,
+                        lhsT=w_codes[g][:, 128 * k : 128 * k + 128].bitcast(E4M3),
+                        lhsT_scale=w_plane[g][:, 128 * k : 128 * k + 128],
+                        rhs=x_codes[:, c0 : c0 + w].bitcast(E4M3),
+                        rhs_scale=x_plane[:, c0 : c0 + w],
+                        start=True,
+                        stop=True,
+                    )
+                banks.append(bank)
+            zs[n] = [banks[j // per][:, j % per, :] for j in range(4)]
+
+        def sa(n, i, j):
+            u, k = slots[n]
+            col = 4 * i + j
+            return coef[:, 4 * UNITS[u][0] + k, col : col + 1]
+
+        def first_products(n):
+            u, k = slots[n]
+            for i in range(4):
+                nc.scalar.activation(out=m_tiles[u][:, i, k, :], in_=zs[n][0], func=COPY, scale=sa(n, i, 0))
+            for i0 in range(0, DISP[n], 2):
+                nd = min(2, DISP[n] - i0)
+                extra = bpool.tile([128, nd, UNITS[u][2]], F32, name="extra")
+                for d in range(nd):
+                    nc.scalar.activation(out=extra[:, d, :], in_=zs[n][1], func=COPY, scale=sa(n, i0 + d, 1))
+                acc = m_tiles[u][:, i0 : i0 + nd, k, :]
+                nc.gpsimd.tensor_tensor(out=acc, in0=acc, in1=extra[:], op=ALU.add)
+
+        def mac(n, i, j):
+            u, k = slots[n]
+            if j == 1 and i < DISP[n]:
+                return
+            acc = m_tiles[u][:, i, k, :]
+            nc.vector.scalar_tensor_tensor(
+                out=acc, in0=zs[n][j], scalar=sa(n, i, j), in1=acc, op0=ALU.mult, op1=ALU.add
+            )
+
+        def macs(ns, rows):
+            for j in range(1, 4):
+                for n in ns:
+                    for i in reversed(rows):
+                        mac(n, i, j)
+
+        kb = [keep.tile([128, UNITS[u][2], 16], BF16, name="kb%d" % u, align_bytes=64) for u in range(3)]
+        o_codes = [keep.tile([128, 4 * UNITS[u][2]], U32, name="o_codes%d" % u, align_bytes=64) for u in range(3)]
+        o_plane = [keep.tile([128, 4 * UNITS[u][2]], U8, name="o_plane%d" % u, align_bytes=64) for u in range(3)]
+
+        def turn_out(u, i, h, on_vector):
+            g, t0, tn = UNITS[u]
+            bank = pst.tile([128, 4, 128], F32, name="tr")
+            for k in range(4):
+                nc.tensor.transpose(bank[:, k, :], m_tiles[u][:, i, k, 128 * h : 128 * h + 128], ident[:])
+            row = opool.tile([128, 128, 4], F32, name="row")
+            src = bank[:].rearrange("p k x -> p x k")
+            if on_vector:
+                nc.vector.tensor_copy(out=row[:], in_=src)
+            else:
+                nc.scalar.copy(out=row[:], in_=src)
+            t1 = t0 + 128 * h
+            nc.sync.dma_start(
+                out=out_0[t1 : t1 + 128, i, 512 * g : 512 * g + 512], in_=row[:].rearrange("p x k -> p (x k)")
+            )
+
+        def cast(u, ip, h, eng):
+            tn = UNITS[u][2]
+            ts = slice(128 * h, 128 * h + 128)
+            src = m_tiles[u][:, 2 * ip : 2 * ip + 2, :, ts].rearrange("p i k (c f) -> p c (i k) f", f=4)
+            dst = kb[u][:, ts, 8 * ip : 8 * ip + 8].rearrange("p (c f) y -> p c y f", f=4)
+            if eng == "g":
+                nc.gpsimd.tensor_scalar(out=dst, in0=src, scalar1=1.0, scalar2=0.0, op0=ALU.mult, op1=ALU.add)
+            elif eng == "s":
+                nc.scalar.copy(out=dst, in_=src)
+            else:
+                nc.vector.tensor_copy(out=dst, in_=src)
+
+        def codes_out(u, h):
+            g, t0, tn = UNITS[u]
+            cols = slice(512 * h, 512 * h + 512)
+            nc.vector.quantize_mx(
+                out=o_codes[u][:, cols].bitcast(E4M3),
+                scales=o_plane[u][:, cols],
+                in_=kb[u][:, 128 * h : 128 * h + 128, :].rearrange("p t y -> p (t y)"),
+            )
+            m0 = 4 * (t0 + 128 * h)
+            nc.sync.dma_start(
+                out=out_1[g].rearrange("p m k -> p (m k)")[:, 4 * m0 : 4 * m0 + 2048].bitcast(I32),
+                in_=o_codes[u][:, cols].bitcast(I32),
+            )
+            for qd in range(4):
+                nc.sync.dma_start(
+                    out=out_2[g, 4 * qd : 4 * qd + 4, m0 : m0 + 512].bitcast(I32),
+                    in_=o_plane[u][32 * qd : 32 * qd + 4, cols].bitcast(I32),
+                )
+
+        ALL = [0, 1, 2, 3]
+        x_turn(0, [0, 1], psz, "z")
+        w_block(0, 0, psz, "z", True)
+        w_block(0, 1, psz, "z", False)
+        w_block(0, 2, psz, "z", True)
+        w_block(0, 3, psz, "z", False)
+        x_turn(1, [0, 1], pst, "tr")
+        x_quant(0, ALL)
+        w_quant(0, 0, 1)
+        x_quant(1, ALL)
+        z_make(0)
+        w_quant(0, 1, 1)
+        w_quant(0, 2, 2)
+        z_make(1)
+        first_products(0)
+        w_block(1, 0, pst, "tr", True)
+        w_block(1, 1, pst, "tr", True)
+        z_make(2)
+        first_products(1)
+        macs([0], ALL)
+        w_block(1, 2, pst, "tr", False)
+        w_block(1, 3, pst, "tr", False)
+        z_make(3)
+        first_products(2)
+        macs([1], ALL)
+        w_quant(1, 0, 4)
+        first_products(3)
+        z_make(4)
+        z_make(5)
+        first_products(4)
+        macs([2], ALL)
+        first_products(5)
+        z_make(6)
+        z_make(7)
+        macs([3], ALL)
+        first_products(6)
+        first_products(7)
+        z_make(8)
+        z_make(9)
+        macs([4, 5], [0, 1])
+        for i in (0, 1):
+            turn_out(0, i, 0, False)
+            turn_out(0, i, 1, False)
+        macs([6, 7], [0, 1])
+        first_products(8)
+        first_products(9)
+        cast(0, 0, 0, "g")
+        cast(0, 0, 1, "g")
+        macs([4, 5], [2, 3])
+        z_make(10)
+        z_make(11)
+        for i in (2, 3):
+            turn_out(0, i, 0, False)
+            turn_out(0, i, 1, False)
+        macs([6, 7], [2, 3])
+        first_products(10)
+        first_products(11)
+        cast(0, 1, 0, "g")
+        cast(0, 1, 1, "g")
+        macs([8, 9], [0, 1])
+        turn_out(1, 0, 0, False)
+        turn_out(1, 1, 0, False)
+        macs([10, 11], [0, 1])
+        cast(1, 0, 0, "g")
+        cast(1, 1, 0, "g")
+        turn_out(1, 2, 0, False)
+        turn_out(1, 3, 0, False)
+        codes_out(0, 0)
+        macs([8, 9], [2, 3])
+        turn_out(2, 0, 0, False)
+        turn_out(2, 1, 0, False)
+        codes_out(0, 1)
+        macs([10, 11], [2, 3])
+        cast(2, 0, 0, "g")
+        codes_out(1, 0)
+        cast(2, 1, 0, "s")
+        turn_out(2, 2, 0, True)
+        turn_out(2, 3, 0, True)
+        codes_out(2, 0)

@@ -17,7 +17,7 @@ T, J, P, R, Q = 256, 4, 512, 512, 1024
 FLOPS = 2 * P * R * Q + 2 * T * J * P * Q + 2 * T * J * J * Q
 
 UNITS = [(0, 0, 256), (1, 0, 128), (1, 128, 128)]
-DISP = [0, 4, 4, 4, 2, 2, 2, 2, 0, 0, 0, 0]
+DISP = [1, 2, 4, 4, 3, 2, 4, 2, 0, 4, 3, 3]
 
 
 def tile_lokrrankgatedkroneckerdelta_x2_kernel(tc, x, a, b, e, c_words, c_scales, s, out_0, out_1, out_2):
@@ -265,81 +265,87 @@ def tile_lokrrankgatedkroneckerdelta_x2_kernel(tc, x, a, b, e, c_words, c_scales
                     in_=o_plane[u][32 * qd : 32 * qd + 4, cols].bitcast(I32),
                 )
 
-        ALL = [0, 1, 2, 3]
-        x_turn(0, [0, 1], psz, "z")
+        x_turn(0, [1], psz, "z")
+        x_turn(1, [0], pst, "tr")
+        w_block(1, 2, pst, "tr", True)
         w_block(0, 0, psz, "z", True)
-        w_block(0, 1, psz, "z", False)
-        w_block(0, 2, psz, "z", True)
-        w_block(0, 3, psz, "z", False)
-        x_turn(1, [0, 1], pst, "tr")
-        x_quant(0, ALL)
-        w_quant(0, 0, 1)
-        x_quant(1, ALL)
-        z_make(0)
+        w_block(0, 1, psz, "z", True)
+        w_block(1, 0, pst, "tr", False)
+        w_block(0, 3, psz, "z", True)
+        w_block(0, 2, psz, "z", False)
+        x_turn(0, [0], psz, "z")
+        x_quant(0, [2, 3])
         w_quant(0, 1, 1)
-        w_quant(0, 2, 2)
-        z_make(1)
-        first_products(0)
-        w_block(1, 0, pst, "tr", True)
-        w_block(1, 1, pst, "tr", True)
-        z_make(2)
-        first_products(1)
-        macs([0], ALL)
-        w_block(1, 2, pst, "tr", False)
+        w_quant(0, 0, 1)
+        x_quant(1, [0, 1])
+        x_turn(1, [1], pst, "tr")
+        x_quant(0, [0, 1])
         w_block(1, 3, pst, "tr", False)
+        x_quant(1, [2, 3])
+        w_quant(0, 2, 2)
+        w_block(1, 1, pst, "tr", True)
+        z_make(0)
+        w_quant(1, 2, 2)
+        first_products(0)
+        z_make(1)
         z_make(3)
-        first_products(2)
-        macs([1], ALL)
-        w_quant(1, 0, 4)
+        w_quant(1, 0, 2)
+        first_products(1)
+        macs([0], [0, 1, 2, 3])
+        macs([1], [0, 1, 2, 3])
         first_products(3)
-        z_make(4)
+        macs([3], [0, 1, 2, 3])
+        z_make(2)
         z_make(5)
-        first_products(4)
-        macs([2], ALL)
-        first_products(5)
-        z_make(6)
+        z_make(4)
         z_make(7)
-        macs([3], ALL)
-        first_products(6)
+        first_products(2)
+        first_products(5)
+        first_products(4)
+        macs([2], [0, 1, 2, 3])
         first_products(7)
-        z_make(8)
-        z_make(9)
-        macs([4, 5], [0, 1])
-        for i in (0, 1):
-            turn_out(0, i, 0, False)
-            turn_out(0, i, 1, False)
-        macs([6, 7], [0, 1])
-        first_products(8)
-        first_products(9)
-        cast(0, 0, 0, "g")
-        cast(0, 0, 1, "g")
-        macs([4, 5], [2, 3])
         z_make(10)
-        z_make(11)
-        for i in (2, 3):
-            turn_out(0, i, 0, False)
-            turn_out(0, i, 1, False)
-        macs([6, 7], [2, 3])
+        macs([4, 5], [0, 1])
         first_products(10)
+        z_make(6)
+        first_products(6)
+        turn_out(0, 3, 1, False)
+        turn_out(0, 0, 0, True)
+        cast(0, 0, 1, "s")
+        macs([4, 5], [2, 3])
+        turn_out(0, 0, 1, False)
+        cast(0, 1, 1, "v")
+        cast(0, 0, 0, "s")
+        macs([6, 7], [2, 3])
+        turn_out(0, 3, 0, False)
+        macs([6, 7], [0, 1])
+        z_make(9)
+        turn_out(0, 2, 1, False)
+        codes_out(0, 1)
+        first_products(9)
+        turn_out(0, 1, 1, False)
+        z_make(11)
+        z_make(8)
+        first_products(8)
+        macs([8, 9], [2, 3])
+        cast(1, 1, 0, "s")
         first_products(11)
-        cast(0, 1, 0, "g")
-        cast(0, 1, 1, "g")
-        macs([8, 9], [0, 1])
-        turn_out(1, 0, 0, False)
+        turn_out(0, 1, 0, False)
+        cast(1, 0, 0, "s")
+        turn_out(0, 2, 0, False)
         turn_out(1, 1, 0, False)
         macs([10, 11], [0, 1])
-        cast(1, 0, 0, "g")
-        cast(1, 1, 0, "g")
-        turn_out(1, 2, 0, False)
+        cast(0, 1, 0, "v")
         turn_out(1, 3, 0, False)
-        codes_out(0, 0)
-        macs([8, 9], [2, 3])
-        turn_out(2, 0, 0, False)
-        turn_out(2, 1, 0, False)
-        codes_out(0, 1)
+        turn_out(1, 0, 0, False)
+        macs([8, 9], [0, 1])
+        turn_out(1, 2, 0, False)
         macs([10, 11], [2, 3])
-        cast(2, 0, 0, "g")
+        turn_out(2, 1, 0, False)
+        turn_out(2, 0, 0, False)
         codes_out(1, 0)
+        codes_out(0, 0)
+        cast(2, 0, 0, "s")
         cast(2, 1, 0, "s")
         turn_out(2, 2, 0, True)
         turn_out(2, 3, 0, True)

@@ -16,8 +16,9 @@ COPY = mybir.ActivationFunctionType.Copy
 T, J, P, R, Q = 256, 4, 512, 512, 1024
 FLOPS = 2 * P * R * Q + 2 * T * J * P * Q + 2 * T * J * J * Q
 
-UNITS = [(0, 0, 256), (1, 0, 128), (1, 128, 128)]
-DISP = [1, 2, 4, 4, 3, 2, 4, 2, 0, 4, 3, 3]
+UNITS = [(0, (0, 1)), (0, (2, 3)), (1, (0, 1)), (1, (2, 3))]
+ROUNDS = [(u, (k,), UNITS[u][1]) for u in range(4) for k in range(4)]
+DISP = [0, 2, 2, 2, 1, 2, 2, 2, 2, 2, 0, 0, 1, 1, 0, 2]
 
 
 def tile_lokrrankgatedkroneckerdelta_x2_kernel(tc, x, a, b, e, c_words, c_scales, s, out_0, out_1, out_2):
@@ -51,8 +52,8 @@ def tile_lokrrankgatedkroneckerdelta_x2_kernel(tc, x, a, b, e, c_words, c_scales
             )
         nc.scalar.dma_start(out=s_col[:], in_=s.rearrange("(g p k) -> p g k", g=2, k=4))
         nc.scalar.dma_start(out=a_row[:], in_=a.rearrange("i j -> (i j)").partition_broadcast(128))
-        for h in range(2):
-            for jp in range(2):
+        for jp in range(2):
+            for h in range(2):
                 two = slice(2 * jp, 2 * jp + 2)
                 nc.sync.dma_start(out=x_in[h][:, two, :], in_=x[128 * h : 128 * h + 128, two, :])
 
@@ -73,53 +74,57 @@ def tile_lokrrankgatedkroneckerdelta_x2_kernel(tc, x, a, b, e, c_words, c_scales
         be_bf = keep.tile([128, 4, 512], BF16, name="be_bf", align_bytes=64)
         be_codes = keep.tile([128, 512], U32, name="be_codes", align_bytes=64)
         be_plane = keep.tile([128, 512], U8, name="be_plane", align_bytes=64)
-        for tp in range(2):
-            bank = psz.tile([128, 2, 2, 128], F32, name="z")
-            for t in range(2):
-                words = b_in[:, 2 * tp + t, :].bitcast(F32)
-                for u in range(2):
-                    nc.tensor.transpose(bank[:, t, u, :], words[:, u::2], ident[:])
-            nc.scalar.copy(out=be_words[:, 2 * tp : 2 * tp + 2, :, :], in_=bank[:].rearrange("p t u m -> p t m u"))
-            two = slice(2 * tp, 2 * tp + 2)
+        def be_gate(t):
+            bank = psz.tile([128, 2, 128], F32, name="z")
+            words = b_in[:, t, :].bitcast(F32)
+            for u in range(2):
+                nc.tensor.transpose(bank[:, u, :], words[:, u::2], ident[:])
+            nc.scalar.copy(out=be_words[:, t, :, :], in_=bank[:].rearrange("p u m -> p m u"))
             nc.vector.tensor_tensor(
-                out=be_bf[:, two, :],
-                in0=be_words[:, two, :, :].rearrange("p t m u -> p (t m u)").bitcast(BF16).rearrange("p (t c) -> p t c", t=2),
-                in1=e_rep[:].rearrange("p m k -> p (m k)").unsqueeze(1).to_broadcast([128, 2, 512]),
+                out=be_bf[:, t, :],
+                in0=be_words[:, t, :, :].rearrange("p m u -> p (m u)").bitcast(BF16),
+                in1=e_rep[:].rearrange("p m k -> p (m k)"),
                 op=ALU.mult,
             )
-        for tp in range(2):
-            two = slice(2 * tp, 2 * tp + 2)
-            cols = slice(256 * tp, 256 * tp + 256)
+
+        def be_quant(t):
             nc.vector.quantize_mx(
-                out=be_codes[:, cols].bitcast(E4M3),
-                scales=be_plane[:, cols],
-                in_=be_bf[:, two, :].rearrange("p t c -> p (t c)"),
+                out=be_codes[:, 128 * t : 128 * t + 128].bitcast(E4M3),
+                scales=be_plane[:, 128 * t : 128 * t + 128],
+                in_=be_bf[:, t, :],
             )
+
+        be_gate(0)
+        for t in range(1, 4):
+            be_gate(t)
+            be_quant(t - 1)
+        be_quant(3)
 
         x_words = keep.tile([128, 4, 256, 2], F32, name="x_words", align_bytes=64)
         x_codes = keep.tile([128, 1024], U32, name="x_codes", align_bytes=64)
         x_plane = keep.tile([128, 1024], U8, name="x_plane", align_bytes=64)
 
-        def x_turn(h, jps, pool, name):
+        def x_turn(h, jps, pool, name, on_vector):
             for jp in jps:
                 bank = pool.tile([128, 2, 2, 128], F32, name=name)
                 for jj in range(2):
                     words = x_in[h][:, 2 * jp + jj, :].bitcast(F32)
                     for u in range(2):
                         nc.tensor.transpose(bank[:, jj, u, :], words[:, u::2], ident[:])
-                nc.scalar.copy(
-                    out=x_words[:, 2 * jp : 2 * jp + 2, 128 * h : 128 * h + 128, :],
-                    in_=bank[:].rearrange("p j u t -> p j t u"),
-                )
+                dst = x_words[:, 2 * jp : 2 * jp + 2, 128 * h : 128 * h + 128, :]
+                src = bank[:].rearrange("p j u t -> p j t u")
+                if on_vector:
+                    nc.vector.tensor_copy(out=dst, in_=src)
+                else:
+                    nc.scalar.copy(out=dst, in_=src)
 
-        def x_quant(h, js):
-            for j in js:
-                c0 = 256 * j + 128 * h
-                nc.vector.quantize_mx(
-                    out=x_codes[:, c0 : c0 + 128].bitcast(E4M3),
-                    scales=x_plane[:, c0 : c0 + 128],
-                    in_=x_words[:, j, 128 * h : 128 * h + 128, :].rearrange("p t u -> p (t u)").bitcast(BF16),
-                )
+        def x_quant(j0, n):
+            cols = slice(256 * j0, 256 * (j0 + n))
+            nc.vector.quantize_mx(
+                out=x_codes[:, cols].bitcast(E4M3),
+                scales=x_plane[:, cols],
+                in_=x_words[:, j0 : j0 + n, :, :].rearrange("p j t u -> p (j t u)").bitcast(BF16),
+            )
 
         w_bf = [keep.tile([128, 4, 128, 4], BF16, name="w_bf%d" % g, align_bytes=64) for g in range(2)]
         w_codes = [keep.tile([128, 512], U32, name="w_codes%d" % g, align_bytes=64) for g in range(2)]
@@ -153,92 +158,94 @@ def tile_lokrrankgatedkroneckerdelta_x2_kernel(tc, x, a, b, e, c_words, c_scales
                 in_=w_bf[g][:, k0 : k0 + n, :, :].rearrange("p k x t -> p (k x t)"),
             )
 
-        slots = [(u, k) for u in range(3) for k in range(4)]
-        m_tiles = [keep.tile([128, 4, 4, UNITS[u][2]], F32, name="m%d" % u) for u in range(3)]
+        m_tiles = [keep.tile([128, len(UNITS[u][1]), 4, 256], F32, name="m%d" % u) for u in range(4)]
         zs = {}
 
-        def z_make(n):
-            u, k = slots[n]
-            g, t0, tn = UNITS[u]
-            per = 512 // tn
-            banks = []
-            for bk in range(4 // per):
-                bank = psz.tile([128, per, tn], F32, name="z")
-                if tn == 256:
-                    c0 = 512 * bk
-                    pieces = [(bank[:].rearrange("p j t -> p (j t)"), c0, 512)]
-                else:
-                    pieces = [(bank[:, j, :], 256 * j + t0, 128) for j in range(4)]
-                for dst, c0, w in pieces:
-                    nc.tensor.matmul_mx(
-                        out=dst,
-                        lhsT=w_codes[g][:, 128 * k : 128 * k + 128].bitcast(E4M3),
-                        lhsT_scale=w_plane[g][:, 128 * k : 128 * k + 128],
-                        rhs=x_codes[:, c0 : c0 + w].bitcast(E4M3),
-                        rhs_scale=x_plane[:, c0 : c0 + w],
-                        start=True,
-                        stop=True,
-                    )
-                banks.append(bank)
-            zs[n] = [banks[j // per][:, j % per, :] for j in range(4)]
+        def z_make(n, jp):
+            u, ks, rows = ROUNDS[n]
+            g = UNITS[u][0]
+            for k in ks:
+                cols = slice(128 * k, 128 * k + 128)
+                bank = psz.tile([128, 2, 256], F32, name="z")
+                nc.tensor.matmul_mx(
+                    out=bank[:].rearrange("p j t -> p (j t)"),
+                    lhsT=w_codes[g][:, cols].bitcast(E4M3),
+                    lhsT_scale=w_plane[g][:, cols],
+                    rhs=x_codes[:, 512 * jp : 512 * jp + 512].bitcast(E4M3),
+                    rhs_scale=x_plane[:, 512 * jp : 512 * jp + 512],
+                    start=True,
+                    stop=True,
+                )
+                zs[n, k, jp] = bank
 
-        def sa(n, i, j):
-            u, k = slots[n]
-            col = 4 * i + j
+        def pieces(n):
+            u, ks, rows = ROUNDS[n]
+            return [(k, ii) for k in ks for ii in range(len(rows))]
+
+        def z_of(n, k, j):
+            return zs[n, k, j // 2][:, j % 2, :]
+
+        def sa(n, k, ii, j):
+            u, ks, rows = ROUNDS[n]
+            col = 4 * rows[ii] + j
             return coef[:, 4 * UNITS[u][0] + k, col : col + 1]
 
         def first_products(n):
-            u, k = slots[n]
-            for i in range(4):
-                nc.scalar.activation(out=m_tiles[u][:, i, k, :], in_=zs[n][0], func=COPY, scale=sa(n, i, 0))
-            for i0 in range(0, DISP[n], 2):
-                nd = min(2, DISP[n] - i0)
-                extra = bpool.tile([128, nd, UNITS[u][2]], F32, name="extra")
-                for d in range(nd):
-                    nc.scalar.activation(out=extra[:, d, :], in_=zs[n][1], func=COPY, scale=sa(n, i0 + d, 1))
-                acc = m_tiles[u][:, i0 : i0 + nd, k, :]
+            m = m_tiles[ROUNDS[n][0]]
+            two = pieces(n)
+            nd = DISP[n]
+            for k, ii in two:
+                nc.scalar.activation(out=m[:, ii, k, :], in_=z_of(n, k, 0), func=COPY, scale=sa(n, k, ii, 0))
+            if nd:
+                extra = bpool.tile([128, nd, 256], F32, name="extra")
+                for d, (k, ii) in enumerate(two[:nd]):
+                    nc.scalar.activation(out=extra[:, d, :], in_=z_of(n, k, 1), func=COPY, scale=sa(n, k, ii, 1))
+                if nd == 2 and len(ROUNDS[n][1]) == 1:
+                    acc = m[:, :, two[0][0], :]
+                elif nd == 2:
+                    acc = m[:, 0, two[0][0] : two[0][0] + 2, :]
+                else:
+                    acc = m[:, two[0][1] : two[0][1] + 1, two[0][0], :]
                 nc.gpsimd.tensor_tensor(out=acc, in0=acc, in1=extra[:], op=ALU.add)
 
-        def mac(n, i, j):
-            u, k = slots[n]
-            if j == 1 and i < DISP[n]:
-                return
-            acc = m_tiles[u][:, i, k, :]
-            nc.vector.scalar_tensor_tensor(
-                out=acc, in0=zs[n][j], scalar=sa(n, i, j), in1=acc, op0=ALU.mult, op1=ALU.add
-            )
+        def macs(n):
+            m = m_tiles[ROUNDS[n][0]]
+            two = pieces(n)
+            terms = [(d, j) for j in range(1, 4) for d in (1, 0) if j > 1 or d >= DISP[n]]
+            if DISP[n] == 1:
+                terms = [(1, 1), (0, 2), (1, 2), (0, 3), (1, 3)]
+            for d, j in terms:
+                k, ii = two[d]
+                acc = m[:, ii, k, :]
+                nc.vector.scalar_tensor_tensor(
+                    out=acc, in0=z_of(n, k, j), scalar=sa(n, k, ii, j), in1=acc, op0=ALU.mult, op1=ALU.add
+                )
 
-        def macs(ns, rows):
-            for j in range(1, 4):
-                for n in ns:
-                    for i in reversed(rows):
-                        mac(n, i, j)
+        kb = [keep.tile([128, 256, 16], BF16, name="kb%d" % g, align_bytes=64) for g in range(2)]
+        o_codes = [keep.tile([128, 1024], U32, name="o_codes%d" % g, align_bytes=64) for g in range(2)]
+        o_plane = [keep.tile([128, 1024], U8, name="o_plane%d" % g, align_bytes=64) for g in range(2)]
 
-        kb = [keep.tile([128, UNITS[u][2], 16], BF16, name="kb%d" % u, align_bytes=64) for u in range(3)]
-        o_codes = [keep.tile([128, 4 * UNITS[u][2]], U32, name="o_codes%d" % u, align_bytes=64) for u in range(3)]
-        o_plane = [keep.tile([128, 4 * UNITS[u][2]], U8, name="o_plane%d" % u, align_bytes=64) for u in range(3)]
-
-        def turn_out(u, i, h, on_vector):
-            g, t0, tn = UNITS[u]
+        def turn_out(u, ii, h, on_vector):
+            g, i = UNITS[u][0], UNITS[u][1][ii]
             bank = pst.tile([128, 4, 128], F32, name="tr")
             for k in range(4):
-                nc.tensor.transpose(bank[:, k, :], m_tiles[u][:, i, k, 128 * h : 128 * h + 128], ident[:])
+                nc.tensor.transpose(bank[:, k, :], m_tiles[u][:, ii, k, 128 * h : 128 * h + 128], ident[:])
             row = opool.tile([128, 128, 4], F32, name="row")
             src = bank[:].rearrange("p k x -> p x k")
             if on_vector:
                 nc.vector.tensor_copy(out=row[:], in_=src)
             else:
                 nc.scalar.copy(out=row[:], in_=src)
-            t1 = t0 + 128 * h
             nc.sync.dma_start(
-                out=out_0[t1 : t1 + 128, i, 512 * g : 512 * g + 512], in_=row[:].rearrange("p x k -> p (x k)")
+                out=out_0[128 * h : 128 * h + 128, i, 512 * g : 512 * g + 512],
+                in_=row[:].rearrange("p x k -> p (x k)"),
             )
 
-        def cast(u, ip, h, eng):
-            tn = UNITS[u][2]
+        def cast(u, h, eng):
+            g, rows = UNITS[u]
             ts = slice(128 * h, 128 * h + 128)
-            src = m_tiles[u][:, 2 * ip : 2 * ip + 2, :, ts].rearrange("p i k (c f) -> p c (i k) f", f=4)
-            dst = kb[u][:, ts, 8 * ip : 8 * ip + 8].rearrange("p (c f) y -> p c y f", f=4)
+            src = m_tiles[u][:, :, :, ts].rearrange("p i k (c f) -> p c (i k) f", f=4)
+            dst = kb[g][:, ts, 4 * rows[0] : 4 * rows[0] + 4 * len(rows)].rearrange("p (c f) y -> p c y f", f=4)
             if eng == "g":
                 nc.gpsimd.tensor_scalar(out=dst, in0=src, scalar1=1.0, scalar2=0.0, op0=ALU.mult, op1=ALU.add)
             elif eng == "s":
@@ -246,107 +253,130 @@ def tile_lokrrankgatedkroneckerdelta_x2_kernel(tc, x, a, b, e, c_words, c_scales
             else:
                 nc.vector.tensor_copy(out=dst, in_=src)
 
-        def codes_out(u, h):
-            g, t0, tn = UNITS[u]
+        def codes_out(g, h):
             cols = slice(512 * h, 512 * h + 512)
             nc.vector.quantize_mx(
-                out=o_codes[u][:, cols].bitcast(E4M3),
-                scales=o_plane[u][:, cols],
-                in_=kb[u][:, 128 * h : 128 * h + 128, :].rearrange("p t y -> p (t y)"),
+                out=o_codes[g][:, cols].bitcast(E4M3),
+                scales=o_plane[g][:, cols],
+                in_=kb[g][:, 128 * h : 128 * h + 128, :].rearrange("p t y -> p (t y)"),
             )
-            m0 = 4 * (t0 + 128 * h)
             nc.sync.dma_start(
-                out=out_1[g].rearrange("p m k -> p (m k)")[:, 4 * m0 : 4 * m0 + 2048].bitcast(I32),
-                in_=o_codes[u][:, cols].bitcast(I32),
+                out=out_1[g].rearrange("p m k -> p (m k)")[:, 2048 * h : 2048 * h + 2048].bitcast(I32),
+                in_=o_codes[g][:, cols].bitcast(I32),
             )
             for qd in range(4):
                 nc.sync.dma_start(
-                    out=out_2[g, 4 * qd : 4 * qd + 4, m0 : m0 + 512].bitcast(I32),
-                    in_=o_plane[u][32 * qd : 32 * qd + 4, cols].bitcast(I32),
+                    out=out_2[g, 4 * qd : 4 * qd + 4, cols].bitcast(I32),
+                    in_=o_plane[g][32 * qd : 32 * qd + 4, cols].bitcast(I32),
                 )
 
-        x_turn(0, [1], psz, "z")
-        x_turn(1, [0], pst, "tr")
-        w_block(1, 2, pst, "tr", True)
-        w_block(0, 0, psz, "z", True)
-        w_block(0, 1, psz, "z", True)
-        w_block(1, 0, pst, "tr", False)
-        w_block(0, 3, psz, "z", True)
-        w_block(0, 2, psz, "z", False)
-        x_turn(0, [0], psz, "z")
-        x_quant(0, [2, 3])
-        w_quant(0, 1, 1)
+        x_turn(0, [0], psz, "z", False)
+        x_turn(1, [0], psz, "z", False)
+        w_block(0, 0, pst, "tr", True)
+        w_block(0, 1, pst, "tr", False)
+        w_block(0, 2, psz, "z", True)
+        w_block(0, 3, psz, "z", False)
+        x_quant(0, 2)
         w_quant(0, 0, 1)
-        x_quant(1, [0, 1])
-        x_turn(1, [1], pst, "tr")
-        x_quant(0, [0, 1])
-        w_block(1, 3, pst, "tr", False)
-        x_quant(1, [2, 3])
+        x_turn(0, [1], pst, "tr", False)
+        x_turn(1, [1], pst, "tr", False)
+        z_make(0, 0)
+        w_quant(0, 1, 1)
         w_quant(0, 2, 2)
-        w_block(1, 1, pst, "tr", True)
-        z_make(0)
-        w_quant(1, 2, 2)
+        z_make(1, 0)
         first_products(0)
-        z_make(1)
-        z_make(3)
-        w_quant(1, 0, 2)
+        x_quant(2, 2)
+        z_make(0, 1)
+        z_make(1, 1)
         first_products(1)
-        macs([0], [0, 1, 2, 3])
-        macs([1], [0, 1, 2, 3])
-        first_products(3)
-        macs([3], [0, 1, 2, 3])
-        z_make(2)
-        z_make(5)
-        z_make(4)
-        z_make(7)
+        z_make(2, 0)
+        z_make(2, 1)
         first_products(2)
-        first_products(5)
+        macs(0)
+        w_block(1, 1, pst, "tr", True)
+        z_make(3, 0)
+        z_make(3, 1)
+        first_products(3)
+        macs(1)
+        w_block(1, 0, pst, "tr", False)
+        w_block(1, 3, pst, "tr", False)
+        z_make(4, 0)
+        z_make(4, 1)
         first_products(4)
-        macs([2], [0, 1, 2, 3])
-        first_products(7)
-        z_make(10)
-        macs([4, 5], [0, 1])
-        first_products(10)
-        z_make(6)
+        macs(2)
+        w_block(1, 2, pst, "tr", True)
+        z_make(5, 0)
+        z_make(5, 1)
+        first_products(5)
+        macs(3)
+        z_make(6, 0)
+        z_make(6, 1)
         first_products(6)
-        turn_out(0, 3, 1, False)
-        turn_out(0, 0, 0, True)
-        cast(0, 0, 1, "s")
-        macs([4, 5], [2, 3])
+        macs(4)
+        w_quant(1, 0, 4)
         turn_out(0, 0, 1, False)
-        cast(0, 1, 1, "v")
-        cast(0, 0, 0, "s")
-        macs([6, 7], [2, 3])
-        turn_out(0, 3, 0, False)
-        macs([6, 7], [0, 1])
-        z_make(9)
-        turn_out(0, 2, 1, False)
-        codes_out(0, 1)
-        first_products(9)
-        turn_out(0, 1, 1, False)
-        z_make(11)
-        z_make(8)
+        z_make(7, 0)
+        z_make(7, 1)
+        first_products(7)
+        macs(5)
+        z_make(8, 0)
+        z_make(8, 1)
         first_products(8)
-        macs([8, 9], [2, 3])
-        cast(1, 1, 0, "s")
-        first_products(11)
-        turn_out(0, 1, 0, False)
-        cast(1, 0, 0, "s")
-        turn_out(0, 2, 0, False)
+        macs(6)
+        z_make(9, 0)
+        z_make(9, 1)
+        first_products(9)
+        macs(7)
+        turn_out(0, 0, 0, False)
         turn_out(1, 1, 0, False)
-        macs([10, 11], [0, 1])
-        cast(0, 1, 0, "v")
-        turn_out(1, 3, 0, False)
+        turn_out(1, 1, 1, False)
+        cast(1, 0, "g")
+        z_make(10, 0)
+        z_make(10, 1)
+        first_products(10)
+        macs(8)
+        cast(0, 1, "g")
+        z_make(11, 0)
+        z_make(11, 1)
+        first_products(11)
+        macs(9)
+        z_make(12, 0)
+        z_make(12, 1)
+        first_products(12)
+        macs(10)
         turn_out(1, 0, 0, False)
-        macs([8, 9], [0, 1])
-        turn_out(1, 2, 0, False)
-        macs([10, 11], [2, 3])
-        turn_out(2, 1, 0, False)
+        turn_out(1, 0, 1, False)
+        z_make(13, 0)
+        z_make(13, 1)
+        first_products(13)
+        macs(11)
+        turn_out(0, 1, 0, False)
+        turn_out(2, 0, 1, False)
+        z_make(14, 0)
+        z_make(14, 1)
+        first_products(14)
+        macs(12)
+        cast(2, 1, "g")
+        z_make(15, 0)
+        z_make(15, 1)
+        first_products(15)
+        macs(13)
         turn_out(2, 0, 0, False)
-        codes_out(1, 0)
+        macs(14)
+        turn_out(0, 1, 1, False)
+        cast(0, 0, "s")
+        macs(15)
+        turn_out(2, 1, 0, False)
+        turn_out(2, 1, 1, False)
+        cast(1, 1, "g")
         codes_out(0, 0)
-        cast(2, 0, 0, "s")
-        cast(2, 1, 0, "s")
-        turn_out(2, 2, 0, True)
-        turn_out(2, 3, 0, True)
-        codes_out(2, 0)
+        cast(2, 0, "s")
+        codes_out(0, 1)
+        turn_out(3, 0, 0, False)
+        turn_out(3, 0, 1, False)
+        turn_out(3, 1, 0, False)
+        cast(3, 0, "v")
+        codes_out(1, 0)
+        turn_out(3, 1, 1, False)
+        cast(3, 1, "g")
+        codes_out(1, 1)

@@ -18,7 +18,7 @@ FLOPS = 2 * P * R * Q + 2 * T * J * P * Q + 2 * T * J * J * Q
 
 UNITS = [(0, (0, 1)), (0, (2, 3)), (1, (0, 1)), (1, (2, 3))]
 ROUNDS = [(u, (k,), UNITS[u][1]) for u in range(4) for k in range(4)]
-DISP = [0, 2, 2, 2, 1, 2, 2, 2, 2, 2, 0, 0, 1, 1, 0, 2]
+DISP = [0, 2, 1, 1, 2, 2, 2, 1, 2, 1, 2, 1, 0, 0, 2, 1]
 
 
 def tile_lokrrankgatedkroneckerdelta_x2_kernel(tc, x, a, b, e, c_words, c_scales, s, out_0, out_1, out_2):
@@ -38,37 +38,30 @@ def tile_lokrrankgatedkroneckerdelta_x2_kernel(tc, x, a, b, e, c_words, c_scales
         a_row = keep.tile([128, 16], BF16, name="a_row")
         c_codes = keep.tile([128, 2 * Q], U8, name="c_codes", align_bytes=64)
         c_plane = keep.tile([128, Q], U8, name="c_plane", align_bytes=64)
-        x_in = [keep.tile([128, 4, 512], BF16, name="x_in%d" % h) for h in range(2)]
+        x_in = keep.tile([128, 2, 4, 512], BF16, name="x_in")
 
+        nc.scalar.dma_start(out=e_col[:], in_=e.rearrange("(p k) -> p k", k=4))
         nc.vector.memset(c_plane[:].bitcast(I32), 0)
         nc.sync.dma_start(out=b_in[:, 0:2, :], in_=b_src[:, 0:2, :])
         nc.sync.dma_start(out=b_in[:, 2:4, :], in_=b_src[:, 2:4, :])
-        nc.scalar.dma_start(out=e_col[:], in_=e.rearrange("(p k) -> p k", k=4))
-        nc.sync.dma_start(out=c_codes[:].bitcast(I32), in_=c_words[0].bitcast(I32))
         for qd in range(4):
             nc.scalar.dma_start(
                 out=c_plane[32 * qd : 32 * qd + 4, :].bitcast(I32),
                 in_=c_scales[0, 4 * qd : 4 * qd + 4, :].bitcast(I32),
             )
-        nc.scalar.dma_start(out=s_col[:], in_=s.rearrange("(g p k) -> p g k", g=2, k=4))
-        nc.scalar.dma_start(out=a_row[:], in_=a.rearrange("i j -> (i j)").partition_broadcast(128))
-        for jp in range(2):
-            for h in range(2):
-                two = slice(2 * jp, 2 * jp + 2)
-                nc.sync.dma_start(out=x_in[h][:, two, :], in_=x[128 * h : 128 * h + 128, two, :])
+        x_src = x.rearrange("(h t) j p -> t h j p", h=2)
+        nc.sync.dma_start(out=x_in[:, :, 0:2, :], in_=x_src[:, :, 0:2, :])
+        nc.sync.dma_start(out=c_codes[:].bitcast(I32), in_=c_words[0].bitcast(I32))
+        nc.sync.dma_start(out=x_in[:, :, 2:4, :], in_=x_src[:, :, 2:4, :])
 
         ident = keep.tile([128, 128], F32, name="ident")
         make_identity(nc, ident[:])
+        nc.gpsimd.dma_start(out=s_col[:], in_=s.rearrange("(g p k) -> p g k", g=2, k=4))
+        nc.gpsimd.dma_start(out=a_row[:], in_=a.rearrange("i j -> (i j)").partition_broadcast(128))
 
         e_rep = keep.tile([128, 128, 4], BF16, name="e_rep")
         nc.vector.tensor_copy(out=e_rep[:], in_=e_col[:].unsqueeze(1).to_broadcast([128, 128, 4]))
         coef = keep.tile([128, 8, 16], F32, name="coef")
-        nc.vector.tensor_tensor(
-            out=coef[:],
-            in0=s_col[:].rearrange("p g k -> p (g k)").unsqueeze(2).to_broadcast([128, 8, 16]),
-            in1=a_row[:].unsqueeze(1).to_broadcast([128, 8, 16]),
-            op=ALU.mult,
-        )
 
         be_words = keep.tile([128, 4, 128, 2], F32, name="be_words")
         be_bf = keep.tile([128, 4, 512], BF16, name="be_bf", align_bytes=64)
@@ -99,6 +92,12 @@ def tile_lokrrankgatedkroneckerdelta_x2_kernel(tc, x, a, b, e, c_words, c_scales
             be_gate(t)
             be_quant(t - 1)
         be_quant(3)
+        nc.vector.tensor_tensor(
+            out=coef[:],
+            in0=s_col[:].rearrange("p g k -> p (g k)").unsqueeze(2).to_broadcast([128, 8, 16]),
+            in1=a_row[:].unsqueeze(1).to_broadcast([128, 8, 16]),
+            op=ALU.mult,
+        )
 
         x_words = keep.tile([128, 4, 256, 2], F32, name="x_words", align_bytes=64)
         x_codes = keep.tile([128, 1024], U32, name="x_codes", align_bytes=64)
@@ -108,7 +107,7 @@ def tile_lokrrankgatedkroneckerdelta_x2_kernel(tc, x, a, b, e, c_words, c_scales
             for jp in jps:
                 bank = pool.tile([128, 2, 2, 128], F32, name=name)
                 for jj in range(2):
-                    words = x_in[h][:, 2 * jp + jj, :].bitcast(F32)
+                    words = x_in[:, h, 2 * jp + jj, :].bitcast(F32)
                     for u in range(2):
                         nc.tensor.transpose(bank[:, jj, u, :], words[:, u::2], ident[:])
                 dst = x_words[:, 2 * jp : 2 * jp + 2, 128 * h : 128 * h + 128, :]
@@ -225,29 +224,51 @@ def tile_lokrrankgatedkroneckerdelta_x2_kernel(tc, x, a, b, e, c_words, c_scales
         o_codes = [keep.tile([128, 1024], U32, name="o_codes%d" % g, align_bytes=64) for g in range(2)]
         o_plane = [keep.tile([128, 1024], U8, name="o_plane%d" % g, align_bytes=64) for g in range(2)]
 
+        rows_out = {}
+        codes_done = []
+
         def turn_out(u, ii, h, on_vector):
             g, i = UNITS[u][0], UNITS[u][1][ii]
             bank = pst.tile([128, 4, 128], F32, name="tr")
             for k in range(4):
                 nc.tensor.transpose(bank[:, k, :], m_tiles[u][:, ii, k, 128 * h : 128 * h + 128], ident[:])
-            row = opool.tile([128, 128, 4], F32, name="row")
+            if (u, h) not in rows_out:
+                row = opool.tile([128, 2, 128, 4], F32, name="row")
+                rows_out[u, h] = [row]
+            row = rows_out[u, h][0]
+            rows_out[u, h].append(ii)
             src = bank[:].rearrange("p k x -> p x k")
             if on_vector:
-                nc.vector.tensor_copy(out=row[:], in_=src)
+                nc.vector.tensor_copy(out=row[:, ii, :, :], in_=src)
             else:
-                nc.scalar.copy(out=row[:], in_=src)
-            nc.sync.dma_start(
-                out=out_0[128 * h : 128 * h + 128, i, 512 * g : 512 * g + 512],
-                in_=row[:].rearrange("p x k -> p (x k)"),
-            )
+                nc.scalar.copy(out=row[:, ii, :, :], in_=src)
+            if u == 3:
+                nc.sync.dma_start(
+                    out=out_0[128 * h : 128 * h + 128, i, 512 * g : 512 * g + 512],
+                    in_=row[:, ii, :, :].rearrange("p x k -> p (x k)"),
+                )
+            elif len(rows_out[u, h]) == 3:
+                nc.sync.dma_start(
+                    out=out_0[128 * h : 128 * h + 128, i - ii : i - ii + 2, 512 * g : 512 * g + 512],
+                    in_=row[:].rearrange("p i x k -> p i (x k)"),
+                )
 
         def cast(u, h, eng):
             g, rows = UNITS[u]
             ts = slice(128 * h, 128 * h + 128)
-            src = m_tiles[u][:, :, :, ts].rearrange("p i k (c f) -> p c (i k) f", f=4)
-            dst = kb[g][:, ts, 4 * rows[0] : 4 * rows[0] + 4 * len(rows)].rearrange("p (c f) y -> p c y f", f=4)
+            m = m_tiles[u][:, :, :, ts]
+            packed = kb[g][:, ts, 4 * rows[0] : 4 * rows[0] + 4 * len(rows)]
+            src = m.rearrange("p i k (c f) -> p c (i k) f", f=4)
+            dst = packed.rearrange("p (c f) y -> p c y f", f=4)
             if eng == "g":
-                nc.gpsimd.tensor_scalar(out=dst, in0=src, scalar1=1.0, scalar2=0.0, op0=ALU.mult, op1=ALU.add)
+                nc.gpsimd.tensor_scalar(
+                    out=packed.rearrange("p t (i k) -> p i t k", k=4),
+                    in0=m.rearrange("p i k t -> p i t k"),
+                    scalar1=1.0,
+                    scalar2=0.0,
+                    op0=ALU.mult,
+                    op1=ALU.add,
+                )
             elif eng == "s":
                 nc.scalar.copy(out=dst, in_=src)
             else:
@@ -260,15 +281,22 @@ def tile_lokrrankgatedkroneckerdelta_x2_kernel(tc, x, a, b, e, c_words, c_scales
                 scales=o_plane[g][:, cols],
                 in_=kb[g][:, 128 * h : 128 * h + 128, :].rearrange("p t y -> p (t y)"),
             )
-            nc.sync.dma_start(
-                out=out_1[g].rearrange("p m k -> p (m k)")[:, 2048 * h : 2048 * h + 2048].bitcast(I32),
-                in_=o_codes[g][:, cols].bitcast(I32),
-            )
-            for qd in range(4):
+            codes_done.append(g)
+            if g == 1:
                 nc.sync.dma_start(
-                    out=out_2[g, 4 * qd : 4 * qd + 4, cols].bitcast(I32),
-                    in_=o_plane[g][32 * qd : 32 * qd + 4, cols].bitcast(I32),
+                    out=out_1[g].rearrange("p m k -> p (m k)")[:, 2048 * h : 2048 * h + 2048].bitcast(I32),
+                    in_=o_codes[g][:, cols].bitcast(I32),
                 )
+            if codes_done.count(g) == 2:
+                if g == 0:
+                    nc.sync.dma_start(
+                        out=out_1[g].rearrange("p m k -> p (m k)").bitcast(I32), in_=o_codes[g][:].bitcast(I32)
+                    )
+                for qd in range(4):
+                    nc.sync.dma_start(
+                        out=out_2[g, 4 * qd : 4 * qd + 4, :].bitcast(I32),
+                        in_=o_plane[g][32 * qd : 32 * qd + 4, :].bitcast(I32),
+                    )
 
         x_turn(0, [0], psz, "z", False)
         x_turn(1, [0], psz, "z", False)
@@ -293,28 +321,28 @@ def tile_lokrrankgatedkroneckerdelta_x2_kernel(tc, x, a, b, e, c_words, c_scales
         z_make(2, 1)
         first_products(2)
         macs(0)
-        w_block(1, 1, pst, "tr", True)
+        w_block(1, 0, pst, "tr", True)
+        w_block(1, 2, pst, "tr", False)
         z_make(3, 0)
         z_make(3, 1)
         first_products(3)
         macs(1)
-        w_block(1, 0, pst, "tr", False)
-        w_block(1, 3, pst, "tr", False)
+        w_block(1, 1, pst, "tr", False)
         z_make(4, 0)
         z_make(4, 1)
         first_products(4)
         macs(2)
-        w_block(1, 2, pst, "tr", True)
+        w_block(1, 3, pst, "tr", False)
         z_make(5, 0)
         z_make(5, 1)
         first_products(5)
         macs(3)
+        w_quant(1, 0, 4)
         z_make(6, 0)
         z_make(6, 1)
         first_products(6)
         macs(4)
-        w_quant(1, 0, 4)
-        turn_out(0, 0, 1, False)
+        turn_out(0, 0, 0, False)
         z_make(7, 0)
         z_make(7, 1)
         first_products(7)
@@ -323,60 +351,60 @@ def tile_lokrrankgatedkroneckerdelta_x2_kernel(tc, x, a, b, e, c_words, c_scales
         z_make(8, 1)
         first_products(8)
         macs(6)
+        turn_out(0, 1, 0, False)
         z_make(9, 0)
         z_make(9, 1)
         first_products(9)
         macs(7)
-        turn_out(0, 0, 0, False)
-        turn_out(1, 1, 0, False)
-        turn_out(1, 1, 1, False)
-        cast(1, 0, "g")
         z_make(10, 0)
         z_make(10, 1)
         first_products(10)
         macs(8)
-        cast(0, 1, "g")
+        turn_out(1, 0, 0, False)
         z_make(11, 0)
         z_make(11, 1)
         first_products(11)
         macs(9)
+        turn_out(0, 0, 1, False)
+        turn_out(0, 1, 1, False)
         z_make(12, 0)
         z_make(12, 1)
         first_products(12)
         macs(10)
-        turn_out(1, 0, 0, False)
-        turn_out(1, 0, 1, False)
+        turn_out(1, 1, 1, False)
+        cast(1, 0, "g")
+        cast(1, 1, "g")
         z_make(13, 0)
         z_make(13, 1)
         first_products(13)
         macs(11)
-        turn_out(0, 1, 0, False)
-        turn_out(2, 0, 1, False)
+        turn_out(1, 1, 0, False)
         z_make(14, 0)
         z_make(14, 1)
         first_products(14)
         macs(12)
-        cast(2, 1, "g")
+        turn_out(2, 1, 1, False)
         z_make(15, 0)
         z_make(15, 1)
         first_products(15)
         macs(13)
-        turn_out(2, 0, 0, False)
+        turn_out(1, 0, 1, False)
+        cast(0, 1, "s")
         macs(14)
-        turn_out(0, 1, 1, False)
-        cast(0, 0, "s")
+        turn_out(2, 0, 1, False)
         macs(15)
         turn_out(2, 1, 0, False)
-        turn_out(2, 1, 1, False)
-        cast(1, 1, "g")
-        codes_out(0, 0)
-        cast(2, 0, "s")
         codes_out(0, 1)
-        turn_out(3, 0, 0, False)
-        turn_out(3, 0, 1, False)
-        turn_out(3, 1, 0, False)
+        turn_out(2, 0, 0, False)
+        cast(2, 0, "s")
+        cast(2, 1, "s")
+        cast(0, 0, "g")
+        codes_out(0, 0)
+        turn_out(3, 1, 1, True)
+        cast(3, 1, "s")
+        turn_out(3, 0, 0, True)
         cast(3, 0, "v")
+        turn_out(3, 1, 0, True)
         codes_out(1, 0)
-        turn_out(3, 1, 1, False)
-        cast(3, 1, "g")
         codes_out(1, 1)
+        turn_out(3, 0, 1, False)

from contextlib import ExitStack

import concourse.mybir as mybir
from concourse.masks import make_identity

F32 = mybir.dt.float32
BF16 = mybir.dt.bfloat16
I32 = mybir.dt.int32
U32 = mybir.dt.uint32
U8 = mybir.dt.uint8
E4M3 = mybir.dt.float8_e4m3fn_x4
E2M1 = mybir.dt.float4_e2m1fn_x4
ALU = mybir.AluOpType
COPY = mybir.ActivationFunctionType.Copy

T, J, P, R, Q = 256, 4, 512, 512, 1024
FLOPS = 2 * P * R * Q + 2 * T * J * P * Q + 2 * T * J * J * Q

UNITS = [(0, (0, 1)), (0, (2, 3)), (1, (0, 1)), (1, (2, 3))]
ROUNDS = [(u, (k,), UNITS[u][1]) for u in range(4) for k in range(4)]
DISP = [0, 2, 1, 1, 2, 2, 2, 1, 2, 1, 2, 1, 0, 0, 2, 1]


def tile_lokrrankgatedkroneckerdelta_x2_kernel(tc, x, a, b, e, c_words, c_scales, s, out_0, out_1, out_2):
    nc = tc.nc
    with ExitStack() as ctx:
        keep = ctx.enter_context(tc.tile_pool(name="keep", bufs=1))
        opool = ctx.enter_context(tc.tile_pool(name="opool", bufs=8))
        bpool = ctx.enter_context(tc.tile_pool(name="bpool", bufs=4))
        psz = ctx.enter_context(tc.psum_pool(name="psz", bufs=6))
        pst = ctx.enter_context(tc.psum_pool(name="pst", bufs=2))
        ctx.enter_context(tc.manual_schedule())

        b_in = keep.tile([128, 4, 512], BF16, name="b_in")
        b_src = b.rearrange("(m t) r -> m t r", t=4)
        e_col = keep.tile([128, 4], BF16, name="e_col")
        s_col = keep.tile([128, 2, 4], BF16, name="s_col")
        a_row = keep.tile([128, 16], BF16, name="a_row")
        c_codes = keep.tile([128, 2 * Q], U8, name="c_codes", align_bytes=64)
        c_plane = keep.tile([128, Q], U8, name="c_plane", align_bytes=64)
        x_in = keep.tile([128, 2, 4, 512], BF16, name="x_in")

        nc.scalar.dma_start(out=e_col[:], in_=e.rearrange("(p k) -> p k", k=4))
        nc.vector.memset(c_plane[:].bitcast(I32), 0)
        nc.sync.dma_start(out=b_in[:, 0:2, :], in_=b_src[:, 0:2, :])
        nc.sync.dma_start(out=b_in[:, 2:4, :], in_=b_src[:, 2:4, :])
        for qd in range(4):
            nc.scalar.dma_start(
                out=c_plane[32 * qd : 32 * qd + 4, :].bitcast(I32),
                in_=c_scales[0, 4 * qd : 4 * qd + 4, :].bitcast(I32),
            )
        x_src = x.rearrange("(h t) j p -> t h j p", h=2)
        nc.sync.dma_start(out=x_in[:, :, 0:2, :], in_=x_src[:, :, 0:2, :])
        nc.sync.dma_start(out=c_codes[:].bitcast(I32), in_=c_words[0].bitcast(I32))
        nc.sync.dma_start(out=x_in[:, :, 2:4, :], in_=x_src[:, :, 2:4, :])

        ident = keep.tile([128, 128], F32, name="ident")
        make_identity(nc, ident[:])
        nc.gpsimd.dma_start(out=s_col[:], in_=s.rearrange("(g p k) -> p g k", g=2, k=4))
        nc.gpsimd.dma_start(out=a_row[:], in_=a.rearrange("i j -> (i j)").partition_broadcast(128))

        e_rep = keep.tile([128, 128, 4], BF16, name="e_rep")
        nc.vector.tensor_copy(out=e_rep[:], in_=e_col[:].unsqueeze(1).to_broadcast([128, 128, 4]))
        coef = keep.tile([128, 8, 16], F32, name="coef")

        be_words = keep.tile([128, 4, 128, 2], F32, name="be_words")
        be_bf = keep.tile([128, 4, 512], BF16, name="be_bf", align_bytes=64)
        be_codes = keep.tile([128, 512], U32, name="be_codes", align_bytes=64)
        be_plane = keep.tile([128, 512], U8, name="be_plane", align_bytes=64)
        def be_gate(t):
            bank = psz.tile([128, 2, 128], F32, name="z")
            words = b_in[:, t, :].bitcast(F32)
            for u in range(2):
                nc.tensor.transpose(bank[:, u, :], words[:, u::2], ident[:])
            nc.scalar.copy(out=be_words[:, t, :, :], in_=bank[:].rearrange("p u m -> p m u"))
            nc.vector.tensor_tensor(
                out=be_bf[:, t, :],
                in0=be_words[:, t, :, :].rearrange("p m u -> p (m u)").bitcast(BF16),
                in1=e_rep[:].rearrange("p m k -> p (m k)"),
                op=ALU.mult,
            )

        def be_quant(t):
            nc.vector.quantize_mx(
                out=be_codes[:, 128 * t : 128 * t + 128].bitcast(E4M3),
                scales=be_plane[:, 128 * t : 128 * t + 128],
                in_=be_bf[:, t, :],
            )

        be_gate(0)
        for t in range(1, 4):
            be_gate(t)
            be_quant(t - 1)
        be_quant(3)
        nc.vector.tensor_tensor(
            out=coef[:],
            in0=s_col[:].rearrange("p g k -> p (g k)").unsqueeze(2).to_broadcast([128, 8, 16]),
            in1=a_row[:].unsqueeze(1).to_broadcast([128, 8, 16]),
            op=ALU.mult,
        )

        x_words = keep.tile([128, 4, 256, 2], F32, name="x_words", align_bytes=64)
        x_codes = keep.tile([128, 1024], U32, name="x_codes", align_bytes=64)
        x_plane = keep.tile([128, 1024], U8, name="x_plane", align_bytes=64)

        def x_turn(h, jps, pool, name, on_vector):
            for jp in jps:
                bank = pool.tile([128, 2, 2, 128], F32, name=name)
                for jj in range(2):
                    words = x_in[:, h, 2 * jp + jj, :].bitcast(F32)
                    for u in range(2):
                        nc.tensor.transpose(bank[:, jj, u, :], words[:, u::2], ident[:])
                dst = x_words[:, 2 * jp : 2 * jp + 2, 128 * h : 128 * h + 128, :]
                src = bank[:].rearrange("p j u t -> p j t u")
                if on_vector:
                    nc.vector.tensor_copy(out=dst, in_=src)
                else:
                    nc.scalar.copy(out=dst, in_=src)

        def x_quant(j0, n):
            cols = slice(256 * j0, 256 * (j0 + n))
            nc.vector.quantize_mx(
                out=x_codes[:, cols].bitcast(E4M3),
                scales=x_plane[:, cols],
                in_=x_words[:, j0 : j0 + n, :, :].rearrange("p j t u -> p (j t u)").bitcast(BF16),
            )

        w_bf = [keep.tile([128, 4, 128, 4], BF16, name="w_bf%d" % g, align_bytes=64) for g in range(2)]
        w_codes = [keep.tile([128, 512], U32, name="w_codes%d" % g, align_bytes=64) for g in range(2)]
        w_plane = [keep.tile([128, 512], U8, name="w_plane%d" % g, align_bytes=64) for g in range(2)]

        def w_block(g, blk, pool, name, on_vector):
            bank = pool.tile([128, 4, 128], F32, name=name)
            q0 = 512 * g + 128 * blk
            for t in range(4):
                nc.tensor.matmul_mx(
                    out=bank[:, t, :],
                    lhsT=be_codes[:, 128 * t : 128 * t + 128].bitcast(E4M3),
                    lhsT_scale=be_plane[:, 128 * t : 128 * t + 128],
                    rhs=c_codes[:, 2 * q0 : 2 * q0 + 256].bitcast(E2M1),
                    rhs_scale=c_plane[:, q0 : q0 + 128],
                    start=True,
                    stop=True,
                )
            src = bank[:].rearrange("p t (x k) -> p k x t", k=4)
            dst = w_bf[g][:, :, 32 * blk : 32 * blk + 32, :]
            if on_vector:
                nc.vector.tensor_copy(out=dst, in_=src)
            else:
                nc.scalar.copy(out=dst, in_=src)

        def w_quant(g, k0, n):
            cols = slice(128 * k0, 128 * (k0 + n))
            nc.vector.quantize_mx(
                out=w_codes[g][:, cols].bitcast(E4M3),
                scales=w_plane[g][:, cols],
                in_=w_bf[g][:, k0 : k0 + n, :, :].rearrange("p k x t -> p (k x t)"),
            )

        m_tiles = [keep.tile([128, len(UNITS[u][1]), 4, 256], F32, name="m%d" % u) for u in range(4)]
        zs = {}

        def z_make(n, jp):
            u, ks, rows = ROUNDS[n]
            g = UNITS[u][0]
            for k in ks:
                cols = slice(128 * k, 128 * k + 128)
                bank = psz.tile([128, 2, 256], F32, name="z")
                nc.tensor.matmul_mx(
                    out=bank[:].rearrange("p j t -> p (j t)"),
                    lhsT=w_codes[g][:, cols].bitcast(E4M3),
                    lhsT_scale=w_plane[g][:, cols],
                    rhs=x_codes[:, 512 * jp : 512 * jp + 512].bitcast(E4M3),
                    rhs_scale=x_plane[:, 512 * jp : 512 * jp + 512],
                    start=True,
                    stop=True,
                )
                zs[n, k, jp] = bank

        def pieces(n):
            u, ks, rows = ROUNDS[n]
            return [(k, ii) for k in ks for ii in range(len(rows))]

        def z_of(n, k, j):
            return zs[n, k, j // 2][:, j % 2, :]

        def sa(n, k, ii, j):
            u, ks, rows = ROUNDS[n]
            col = 4 * rows[ii] + j
            return coef[:, 4 * UNITS[u][0] + k, col : col + 1]

        def first_products(n):
            m = m_tiles[ROUNDS[n][0]]
            two = pieces(n)
            nd = DISP[n]
            for k, ii in two:
                nc.scalar.activation(out=m[:, ii, k, :], in_=z_of(n, k, 0), func=COPY, scale=sa(n, k, ii, 0))
            if nd:
                extra = bpool.tile([128, nd, 256], F32, name="extra")
                for d, (k, ii) in enumerate(two[:nd]):
                    nc.scalar.activation(out=extra[:, d, :], in_=z_of(n, k, 1), func=COPY, scale=sa(n, k, ii, 1))
                if nd == 2 and len(ROUNDS[n][1]) == 1:
                    acc = m[:, :, two[0][0], :]
                elif nd == 2:
                    acc = m[:, 0, two[0][0] : two[0][0] + 2, :]
                else:
                    acc = m[:, two[0][1] : two[0][1] + 1, two[0][0], :]
                nc.gpsimd.tensor_tensor(out=acc, in0=acc, in1=extra[:], op=ALU.add)

        def macs(n):
            m = m_tiles[ROUNDS[n][0]]
            two = pieces(n)
            terms = [(d, j) for j in range(1, 4) for d in (1, 0) if j > 1 or d >= DISP[n]]
            if DISP[n] == 1:
                terms = [(1, 1), (0, 2), (1, 2), (0, 3), (1, 3)]
            for d, j in terms:
                k, ii = two[d]
                acc = m[:, ii, k, :]
                nc.vector.scalar_tensor_tensor(
                    out=acc, in0=z_of(n, k, j), scalar=sa(n, k, ii, j), in1=acc, op0=ALU.mult, op1=ALU.add
                )

        kb = [keep.tile([128, 256, 16], BF16, name="kb%d" % g, align_bytes=64) for g in range(2)]
        o_codes = [keep.tile([128, 1024], U32, name="o_codes%d" % g, align_bytes=64) for g in range(2)]
        o_plane = [keep.tile([128, 1024], U8, name="o_plane%d" % g, align_bytes=64) for g in range(2)]

        rows_out = {}
        codes_done = []

        def turn_out(u, ii, h, on_vector):
            g, i = UNITS[u][0], UNITS[u][1][ii]
            bank = pst.tile([128, 4, 128], F32, name="tr")
            for k in range(4):
                nc.tensor.transpose(bank[:, k, :], m_tiles[u][:, ii, k, 128 * h : 128 * h + 128], ident[:])
            if (u, h) not in rows_out:
                row = opool.tile([128, 2, 128, 4], F32, name="row")
                rows_out[u, h] = [row]
            row = rows_out[u, h][0]
            rows_out[u, h].append(ii)
            src = bank[:].rearrange("p k x -> p x k")
            if on_vector:
                nc.vector.tensor_copy(out=row[:, ii, :, :], in_=src)
            else:
                nc.scalar.copy(out=row[:, ii, :, :], in_=src)
            if u == 3:
                nc.sync.dma_start(
                    out=out_0[128 * h : 128 * h + 128, i, 512 * g : 512 * g + 512],
                    in_=row[:, ii, :, :].rearrange("p x k -> p (x k)"),
                )
            elif len(rows_out[u, h]) == 3:
                nc.sync.dma_start(
                    out=out_0[128 * h : 128 * h + 128, i - ii : i - ii + 2, 512 * g : 512 * g + 512],
                    in_=row[:].rearrange("p i x k -> p i (x k)"),
                )

        def cast(u, h, eng):
            g, rows = UNITS[u]
            ts = slice(128 * h, 128 * h + 128)
            m = m_tiles[u][:, :, :, ts]
            packed = kb[g][:, ts, 4 * rows[0] : 4 * rows[0] + 4 * len(rows)]
            src = m.rearrange("p i k (c f) -> p c (i k) f", f=4)
            dst = packed.rearrange("p (c f) y -> p c y f", f=4)
            if eng == "g":
                nc.gpsimd.tensor_scalar(
                    out=packed.rearrange("p t (i k) -> p i t k", k=4),
                    in0=m.rearrange("p i k t -> p i t k"),
                    scalar1=1.0,
                    scalar2=0.0,
                    op0=ALU.mult,
                    op1=ALU.add,
                )
            elif eng == "s":
                nc.scalar.copy(out=dst, in_=src)
            else:
                nc.vector.tensor_copy(out=dst, in_=src)

        def codes_out(g, h):
            cols = slice(512 * h, 512 * h + 512)
            nc.vector.quantize_mx(
                out=o_codes[g][:, cols].bitcast(E4M3),
                scales=o_plane[g][:, cols],
                in_=kb[g][:, 128 * h : 128 * h + 128, :].rearrange("p t y -> p (t y)"),
            )
            codes_done.append(g)
            if g == 1:
                nc.sync.dma_start(
                    out=out_1[g].rearrange("p m k -> p (m k)")[:, 2048 * h : 2048 * h + 2048].bitcast(I32),
                    in_=o_codes[g][:, cols].bitcast(I32),
                )
            if codes_done.count(g) == 2:
                if g == 0:
                    nc.sync.dma_start(
                        out=out_1[g].rearrange("p m k -> p (m k)").bitcast(I32), in_=o_codes[g][:].bitcast(I32)
                    )
                for qd in range(4):
                    nc.sync.dma_start(
                        out=out_2[g, 4 * qd : 4 * qd + 4, :].bitcast(I32),
                        in_=o_plane[g][32 * qd : 32 * qd + 4, :].bitcast(I32),
                    )

        x_turn(0, [0], psz, "z", False)
        x_turn(1, [0], psz, "z", False)
        w_block(0, 0, pst, "tr", True)
        w_block(0, 1, pst, "tr", False)
        w_block(0, 2, psz, "z", True)
        w_block(0, 3, psz, "z", False)
        x_quant(0, 2)
        w_quant(0, 0, 1)
        x_turn(0, [1], pst, "tr", False)
        x_turn(1, [1], pst, "tr", False)
        z_make(0, 0)
        w_quant(0, 1, 1)
        w_quant(0, 2, 2)
        z_make(1, 0)
        first_products(0)
        x_quant(2, 2)
        z_make(0, 1)
        z_make(1, 1)
        first_products(1)
        z_make(2, 0)
        z_make(2, 1)
        first_products(2)
        macs(0)
        w_block(1, 0, pst, "tr", True)
        w_block(1, 2, pst, "tr", False)
        z_make(3, 0)
        z_make(3, 1)
        first_products(3)
        macs(1)
        w_block(1, 1, pst, "tr", False)
        z_make(4, 0)
        z_make(4, 1)
        first_products(4)
        macs(2)
        w_block(1, 3, pst, "tr", False)
        z_make(5, 0)
        z_make(5, 1)
        first_products(5)
        macs(3)
        w_quant(1, 0, 4)
        z_make(6, 0)
        z_make(6, 1)
        first_products(6)
        macs(4)
        turn_out(0, 0, 0, False)
        z_make(7, 0)
        z_make(7, 1)
        first_products(7)
        macs(5)
        z_make(8, 0)
        z_make(8, 1)
        first_products(8)
        macs(6)
        turn_out(0, 1, 0, False)
        z_make(9, 0)
        z_make(9, 1)
        first_products(9)
        macs(7)
        z_make(10, 0)
        z_make(10, 1)
        first_products(10)
        macs(8)
        turn_out(1, 0, 0, False)
        z_make(11, 0)
        z_make(11, 1)
        first_products(11)
        macs(9)
        turn_out(0, 0, 1, False)
        turn_out(0, 1, 1, False)
        z_make(12, 0)
        z_make(12, 1)
        first_products(12)
        macs(10)
        turn_out(1, 1, 1, False)
        cast(1, 0, "g")
        cast(1, 1, "g")
        z_make(13, 0)
        z_make(13, 1)
        first_products(13)
        macs(11)
        turn_out(1, 1, 0, False)
        z_make(14, 0)
        z_make(14, 1)
        first_products(14)
        macs(12)
        turn_out(2, 1, 1, False)
        z_make(15, 0)
        z_make(15, 1)
        first_products(15)
        macs(13)
        turn_out(1, 0, 1, False)
        cast(0, 1, "s")
        macs(14)
        turn_out(2, 0, 1, False)
        macs(15)
        turn_out(2, 1, 0, False)
        codes_out(0, 1)
        turn_out(2, 0, 0, False)
        cast(2, 0, "s")
        cast(2, 1, "s")
        cast(0, 0, "g")
        codes_out(0, 0)
        turn_out(3, 1, 1, True)
        cast(3, 1, "s")
        turn_out(3, 0, 0, True)
        cast(3, 0, "v")
        turn_out(3, 1, 0, True)
        codes_out(1, 0)
        codes_out(1, 1)
        turn_out(3, 0, 1, False)
